import numpy as np
import ml_dtypes


def mxq(x, axis, fmt="e4m3"):
    dtype, down = {"e4m3": (ml_dtypes.float8_e4m3fn, 7), "e5m2": (ml_dtypes.float8_e5m2, 14)}[fmt]
    v = np.moveaxis(np.asarray(x, np.float32).astype(ml_dtypes.bfloat16).astype(np.float64), axis, -1)
    blocks = v.reshape(v.shape[:-1] + (-1, 32))
    amax = np.abs(blocks).max(-1, keepdims=True)
    byte = np.maximum(np.where(amax > 0, np.frexp(amax)[1] - 1 + 127, 0) - down, 1)
    scale = np.exp2(byte - 127.0)
    codes = (blocks / scale).astype(np.float32).astype(dtype).astype(np.float64)
    return np.moveaxis((codes * scale).reshape(v.shape), -1, axis)


WIDE = False


def mx_kscale(k):
    if not WIDE:
        return np.ones(k)
    levels = np.array([10, -10, 5, -5, 0])
    if k % 512:
        return np.exp2(np.random.permutation(np.resize(levels, k // 32))).repeat(32)
    a = np.empty((k // 512, 16))
    for p in range(k // 512):
        a[p, :8] = np.random.permutation(np.resize(levels, 8))
        for g in range(8):
            far = levels[np.abs(levels - a[p, g]) >= 10]
            a[p, g + 8] = far[np.random.randint(len(far))]
    return np.exp2(a.ravel()).repeat(32)


def f64(x):
    return np.asarray(x).astype(np.float64)


def striped(idx):
    return np.tile(np.asarray(idx).reshape(-1, 16).T, (8, 1)).astype(np.uint16)


def unstriped(offs):
    return offs[:16].T.reshape(-1).astype(np.int64)


E2M1 = np.array([0.0, 0.5, 1.0, 1.5, 2.0, 3.0, 4.0, 6.0, -0.0, -0.5, -1.0, -1.5, -2.0, -3.0, -4.0, -6.0])


def pack_weight(w, fmt):
    k, n = w.shape
    w = f64(np.asarray(w, np.float32).astype(ml_dtypes.bfloat16)).reshape(k // 32, 32, n)
    amax = np.abs(w).max(1)
    if fmt == "e4m3":
        byte = np.frexp(amax)[1] - 1 + 127 - 7
    else:
        mant, ex = np.frexp(amax / 6.0)
        byte = np.where(mant > 0.5, ex, ex - 1) + 127
    byte = np.clip(np.where(amax > 0, byte, 1), 1, 254)
    scaled = (w * np.exp2(127.0 - byte)[:, None, :]).reshape(k, n).astype(np.float32)
    by_word = np.ascontiguousarray(scaled.reshape(k // 512, 128, 4, n).transpose(0, 1, 3, 2))
    if fmt == "e4m3":
        words = by_word.astype(ml_dtypes.float8_e4m3fn).view(np.uint8)
    else:
        c = by_word.astype(ml_dtypes.float4_e2m1fn).view(np.uint8) & 0xF
        words = (c[..., 0::2] | (c[..., 1::2] << 4)).reshape(k // 512, 128, 2 * n)
    return np.ascontiguousarray(words), np.ascontiguousarray(byte.astype(np.uint8).reshape(k // 512, 16, n))


def unpack_weight(words, scales, fmt):
    g, _, n = scales.shape
    words = np.ascontiguousarray(words).reshape(g, 128, n, -1)
    if fmt == "e4m3":
        vals = words.view(ml_dtypes.float8_e4m3fn).astype(np.float64)
    else:
        nib = np.empty((g, 128, n, 4), np.uint8)
        nib[..., 0::2] = words & 0xF
        nib[..., 1::2] = words >> 4
        vals = E2M1[nib]
    vals = vals * np.repeat(np.exp2(scales.astype(np.float64) - 127.0), 8, axis=1)[..., None]
    return vals.transpose(0, 1, 3, 2).reshape(g * 512, n)


B, N, T, D, DV, NQ = 2, 1024, 4096, 1024, 256, 128
PAGE = 512
DRAFT = 128


def setup_inputs():
    n = np.random.standard_normal
    pages = np.random.permutation(T // PAGE)[:B * N // PAGE]
    idx = (pages[:, None] * PAGE + np.arange(PAGE)[None, :]).reshape(-1)
    s = mx_kscale(D)[:, None]
    u = np.ones(T)
    u[idx] = mx_kscale(B * N)
    r = np.random.uniform(0.5, 2.0, T)
    k = n((D, T)) / s
    v = n((DV, T)) / (u * r)
    kp = pack_weight(k, "e2m1")
    vp = pack_weight(v.T, "e4m3")
    when = np.zeros(T)
    when[idx] = np.concatenate([np.concatenate([np.arange(N - DRAFT), N - DRAFT + np.random.randint(0, 16, DRAFT)]) for b in range(B)])
    return {
        "qT": (n((B, D, NQ)) * s * (1.00 / np.sqrt(D))).astype(np.float32),
        "k_words": np.ascontiguousarray(kp[0].reshape(D // 1024, 2, 128, T, 2).transpose(0, 2, 3, 1, 4)).reshape(D // 1024, 128, T, 4),
        "k_scales": kp[1],
        "v_words": vp[0],
        "v_scales": vp[1],
        "vs": np.tile(u * r, (128, 1)).astype(np.float32),
        "pos": np.tile(when, (128, 1)).astype(np.float32),
        "qpos": np.random.randint(N - DRAFT, N - DRAFT + 16, (B, NQ, 1)).astype(np.float32),
        "og": n((B, NQ, DV)).astype(np.float32),
        "offs": striped(idx),
        "voffs": striped((pages[:, None] * DV + np.arange(DV)[None, :]).reshape(-1)),
    }


def reference(qT, k_words, k_scales, v_words, v_scales, vs, pos, qpos, og, offs, voffs):
    idx = unstriped(offs)
    k = unpack_weight(k_words.reshape(D // 1024, 128, T, 2, 2).transpose(0, 3, 1, 2, 4).reshape(D // 512, 128, 2 * T), k_scales, "e2m1")
    v = unpack_weight(v_words, v_scales, "e4m3")
    v = v.reshape(T // 512, 512, DV)[unstriped(voffs)[::DV] // DV].reshape(B, N, DV)
    pick = lambda x: x[:, idx].reshape(x.shape[0], B, N).transpose(1, 0, 2)
    q = f64(qT)
    score = mxq(q, 1, "e4m3").transpose(0, 2, 1) @ pick(k)
    score = np.where(pick(f64(pos))[:, :1, :] <= f64(qpos), score, -30000.0)
    m = score.max(-1, keepdims=True)
    p = np.exp(score - m)
    total = p.sum(-1, keepdims=True)
    w = p * pick(f64(vs))[:, :1, :]
    y = mxq(w, 2, "e4m3") @ v
    y = y / total
    y = y / (1.0 + np.exp(-f64(og)))
    return y

@@ -1,0 +1,245 @@
+from contextlib import ExitStack
+
+import concourse.mybir as mybir
+from concourse.masks import make_identity
+
+B, N, T, D, DV, NQ = 2, 1024, 4096, 1024, 256, 128
+PAGE = 512
+P = 128
+PACK = 4
+PASSES = D // PAGE
+PAGES = N // PAGE
+POOL_PAGES = T // PAGE
+LIST_ROWS = 16
+MASKED = 30000.0
+STEEP = 2.0 ** 64
+
+FLOPS = 2 * B * NQ * N * (D + DV)
+
+F32 = mybir.dt.float32
+BF16 = mybir.dt.bfloat16
+I32 = mybir.dt.int32
+U32 = mybir.dt.uint32
+U16 = mybir.dt.uint16
+U8 = mybir.dt.uint8
+FP8X4 = mybir.dt.float8_e4m3fn_x4
+FP4X4 = mybir.dt.float4_e2m1fn_x4
+ALU = mybir.AluOpType
+ACT = mybir.ActivationFunctionType
+
+
+def tile_attend_pkv4_soft_draft_gate_kernel(
+    tc, qT, k_words, k_scales, v_words, v_scales, vs, pos, qpos, og, offs, voffs, out
+):
+    nc = tc.nc
+    with ExitStack() as ctx:
+        keep = ctx.enter_context(tc.tile_pool(name="keep", bufs=1))
+        psum = ctx.enter_context(tc.psum_pool(name="psum", bufs=1))
+
+        def sb(name, shape, dtype):
+            return keep.tile(shape, dtype, name=name, align_bytes=64)
+
+        key_list = keep.tile([P, B * N // LIST_ROWS], U16, name="key_list")
+        value_list = keep.tile([P, B * PAGES * DV // LIST_ROWS], U16, name="value_list")
+        nc.sync.dma_start(value_list[:], voffs)
+        nc.sync.dma_start(key_list[:], offs)
+
+        def keys_of(b):
+            cols = N // LIST_ROWS
+            return key_list[:, b * cols : (b + 1) * cols]
+
+        def values_of(b):
+            cols = PAGES * DV // LIST_ROWS
+            return value_list[:, b * cols : (b + 1) * cols]
+
+        kw_pool = sb("kw_pool", [P, T], U32)
+        ks_pool = sb("ks_pool", [P, T], U8)
+        vw_pool = sb("vw_pool", [P, POOL_PAGES * DV], U32)
+        vsc_pool = sb("vsc_pool", [P, POOL_PAGES * DV], U8)
+        vs_pool = sb("vs_pool", [P, T], F32)
+        pos_pool = sb("pos_pool", [P, T], F32)
+        q_raw = sb("q_raw", [P, B * PASSES, PACK, NQ], F32)
+        og_sb = sb("og_sb", [P, B, DV], F32)
+        qpos_sb = [sb(f"qpos{b}", [P, 1], F32) for b in range(B)]
+        ks_high = [sb(f"ks_high{b}", [P, N], U8) for b in range(B)]
+
+        nc.vector.memset(ks_pool[:].bitcast(I32), 0)
+        nc.vector.memset(vsc_pool[:].bitcast(I32), 0)
+        ident = sb("ident", [P, P], F32)
+        make_identity(nc, ident[:])
+        for b in range(B):
+            nc.gpsimd.memset(ks_high[b][:].bitcast(I32), 0)
+
+        nc.sync.dma_start(
+            vw_pool[:].bitcast(I32).rearrange("p (u e) -> p u e", u=POOL_PAGES),
+            v_words.rearrange("u p e r -> p u (e r)").bitcast(I32),
+        )
+        for quad in range(4):
+            nc.sync.dma_start(
+                ks_pool[32 * quad : 32 * quad + 4 * PASSES, :].bitcast(I32),
+                k_scales[:, 4 * quad : 4 * quad + 4, :].bitcast(I32),
+            )
+        nc.sync.dma_start(
+            kw_pool[:].bitcast(I32), k_words[0].rearrange("p t r -> p (t r)").bitcast(I32)
+        )
+        nc.sync.dma_start(
+            q_raw[:].rearrange("p c j q -> p c (j q)"),
+            qT.rearrange("b (g p j) q -> p (b g) (j q)", g=PASSES, j=PACK),
+        )
+        nc.sync.dma_start(pos_pool[:], pos)
+        for b in range(B):
+            nc.sync.dma_start(qpos_sb[b][:], qpos[b])
+        nc.sync.dma_start(vs_pool[:], vs)
+        nc.sync.dma_start(og_sb[:], og.rearrange("b q e -> q b e"))
+        for quad in range(4):
+            nc.sync.dma_start(
+                vsc_pool[32 * quad : 32 * quad + 4, :].bitcast(I32).rearrange("f (u e) -> f u e", u=POOL_PAGES),
+                v_scales[:, 4 * quad : 4 * quad + 4, :].rearrange("u f e -> f u e").bitcast(I32),
+            )
+
+        vw = sb("vw", [P, B * PAGES * DV], U32)
+        nc.vector.tensor_copy(vw[:], vw_pool[:].indirect(value_list[:]))
+
+        ks = [sb(f"ks{b}", [P, N], U8) for b in range(B)]
+        for b in range(B):
+            nc.vector.tensor_copy(ks[b][:], ks_pool[:].indirect(keys_of(b)))
+            nc.scalar.dma_start(ks_high[b][0:112, :].bitcast(I32), ks[b][4:116, :].bitcast(I32))
+
+        q_bf = sb("q_bf", [P, B * PASSES, NQ, PACK], BF16)
+        for c in range(B * PASSES):
+            nc.scalar.copy(
+                q_bf[:, c].rearrange("p (a i) j -> p a j i", i=4),
+                q_raw[:, c].rearrange("p j (a i) -> p a j i", i=4),
+            )
+        q_codes = sb("q_codes", [P, B * PASSES * NQ], U32)
+        q_scales = sb("q_scales", [P, B * PASSES * NQ], U8)
+
+        kw = [sb(f"kw{b}", [P, N], U32) for b in range(B)]
+        k4 = [sb(f"k4_{b}", [P, PASSES, 2 * N], U8) for b in range(B)]
+        scores = [[psum.tile([P, PAGE], F32, name=f"scores{b}{h}") for h in range(PAGES)] for b in range(B)]
+
+        def gather_keys(b):
+            nc.vector.tensor_copy(kw[b][:], kw_pool[:].indirect(keys_of(b)))
+            nc.vector.tensor_copy(
+                k4[b][:].bitcast(U16),
+                kw[b][:].bitcast(U16).rearrange("p (n g) -> p g n", g=PASSES),
+            )
+
+        def score(b):
+            planes = [ks[b], ks_high[b]]
+            for h in range(PAGES):
+                for g in range(PASSES):
+                    cols = slice((b * PASSES + g) * NQ, (b * PASSES + g + 1) * NQ)
+                    nc.tensor.matmul_mx(
+                        out=scores[b][h][:],
+                        lhsT=q_codes[:, cols].bitcast(FP8X4),
+                        lhsT_scale=q_scales[:, cols],
+                        rhs=k4[b][:, g, 2 * PAGE * h : 2 * PAGE * (h + 1)].bitcast(FP4X4),
+                        rhs_scale=planes[g][:, PAGE * h : PAGE * (h + 1)],
+                        start=(g == 0),
+                        stop=(g == PASSES - 1),
+                    )
+
+        gather_keys(0)
+        nc.vector.quantize_mx(
+            out=q_codes[:].bitcast(FP8X4), scales=q_scales[:], in_=q_bf[:].rearrange("p c q j -> p (c q j)")
+        )
+        score(0)
+        gather_keys(1)
+        score(1)
+
+        ahead = []
+        for b in range(B):
+            places = sb(f"places{b}", [P, N], F32)
+            nc.vector.tensor_copy(places[:], pos_pool[:].indirect(keys_of(b)))
+            origin = sb(f"origin{b}", [P, 1], F32)
+            nc.scalar.mul(origin[:], qpos_sb[b][:], -STEEP)
+            pen = sb(f"ahead{b}", [P, N], F32)
+            nc.scalar.activation(pen[:], places[:], ACT.Relu, bias=origin[:], scale=STEEP)
+            ahead.append(pen)
+
+        gate = sb("gate", [P, B, DV], F32)
+        half = sb("half", [P, B, DV], F32)
+        nc.scalar.activation(half[:], og_sb[:], ACT.Tanh, scale=0.5)
+        nc.scalar.activation(gate[:], half[:], ACT.Copy, bias=0.5, scale=0.5)
+
+        p = [sb(f"p{b}", [P, N], F32) for b in range(B)]
+        sums = [sb(f"sums{b}", [P, PAGES], F32) for b in range(B)]
+        sizes = [sb(f"sizes{b}", [P, N], F32) for b in range(B)]
+        vsc = [sb(f"vsc{b}", [P, PAGES * DV], U8) for b in range(B)]
+        w = [[sb(f"w{b}{h}", [P, PAGE], BF16) for h in range(PAGES)] for b in range(B)]
+        wt = [[sb(f"wt{b}{h}", [P, NQ, PACK], BF16) for h in range(PAGES)] for b in range(B)]
+        y = [psum.tile([P, DV], F32, name=f"y{b}") for b in range(B)]
+
+        def softmax(b):
+            low = sb(f"low{b}", [P, N], F32)
+            for h in range(PAGES):
+                cols = slice(PAGE * h, PAGE * (h + 1))
+                nc.vector.tensor_tensor(low[:, cols], ahead[b][:, cols], scores[b][h][:], ALU.subtract)
+            neg = sb(f"neg{b}", [P, N], F32)
+            neg_max = sb(f"neg_max{b}", [P, 1], F32)
+            nc.vector.tensor_scalar(neg[:], low[:], MASKED, None, ALU.min, ALU.min, accum_out=neg_max[:])
+            for h in range(PAGES):
+                cols = slice(PAGE * h, PAGE * (h + 1))
+                nc.scalar.activation(
+                    p[b][:, cols], neg[:, cols], ACT.Exp, bias=neg_max[:], scale=-1.0, accum_out=sums[b][:, h : h + 1]
+                )
+
+        def gather_sizes(b):
+            nc.vector.tensor_copy(sizes[b][:], vs_pool[:].indirect(keys_of(b)))
+
+        def gather_value_scales(b):
+            nc.vector.tensor_copy(vsc[b][:], vsc_pool[:].indirect(values_of(b)))
+
+        def weigh(b):
+            for h in range(PAGES):
+                cols = slice(PAGE * h, PAGE * (h + 1))
+                nc.vector.tensor_tensor(w[b][h][:], p[b][:, cols], sizes[b][:, cols], ALU.mult)
+                pairs = w[b][h][:].bitcast(F32)
+                turned = psum.tile([P, 2, NQ], F32, name=f"turned{h}")
+                for u in range(2):
+                    nc.tensor.transpose(turned[:, u, :], pairs[:, u : PAGE // 2 : 2], ident[:])
+                nc.scalar.copy(
+                    wt[b][h][:].rearrange("p q j -> p (q j)").bitcast(F32).rearrange("p (q u) -> p q u", u=2),
+                    turned[:].rearrange("p u q -> p q u"),
+                )
+
+        def multiply(b):
+            for h in range(PAGES):
+                w_codes = sb(f"w_codes{b}{h}", [P, NQ], U32)
+                w_scales = sb(f"w_scales{b}{h}", [P, NQ], U8)
+                nc.vector.quantize_mx(
+                    out=w_codes[:].bitcast(FP8X4), scales=w_scales[:], in_=wt[b][h][:].rearrange("p q j -> p (q j)")
+                )
+                page = b * PAGES + h
+                nc.tensor.matmul_mx(
+                    out=y[b][:],
+                    lhsT=w_codes[:].bitcast(FP8X4),
+                    lhsT_scale=w_scales[:],
+                    rhs=vw[:, page * DV : (page + 1) * DV].bitcast(FP8X4),
+                    rhs_scale=vsc[b][:, h * DV : (h + 1) * DV],
+                    start=(h == 0),
+                    stop=(h == PAGES - 1),
+                )
+
+        def finish(b):
+            total = sb(f"total{b}", [P, 1], F32)
+            nc.scalar.activation(total[:], sums[b][:, 0:1], ACT.Identity, bias=sums[b][:, 1:2])
+            inverse = sb(f"inverse{b}", [P, 1], F32)
+            nc.vector.reciprocal(inverse[:], total[:])
+            result = sb(f"result{b}", [P, DV], F32)
+            nc.vector.scalar_tensor_tensor(result[:], y[b][:], inverse[:], gate[:, b, :], ALU.mult, ALU.mult)
+            nc.sync.dma_start(out[b], result[:])
+
+        softmax(0)
+        gather_sizes(0)
+        softmax(1)
+        weigh(0)
+        gather_sizes(1)
+        gather_value_scales(0)
+        multiply(0)
+        weigh(1)
+        gather_value_scales(1)
+        finish(0)
+        multiply(1)
+        finish(1)

@@ -1,7 +1,6 @@
 from contextlib import ExitStack
 
 import concourse.mybir as mybir
-from concourse.masks import make_identity
 
 B, N, T, D, DV, NQ = 2, 1024, 4096, 1024, 256, 128
 PAGE = 512
@@ -36,8 +35,8 @@ def tile_attend_pkv4_soft_draft_gate_kernel(
         keep = ctx.enter_context(tc.tile_pool(name="keep", bufs=1))
         psum = ctx.enter_context(tc.psum_pool(name="psum", bufs=1))
 
-        def sb(name, shape, dtype):
-            return keep.tile(shape, dtype, name=name, align_bytes=64)
+        def sb(name, shape, dtype, tag=None):
+            return keep.tile(shape, dtype, name=name, tag=tag or name, align_bytes=64)
 
         key_list = keep.tile([P, B * N // LIST_ROWS], U16, name="key_list")
         value_list = keep.tile([P, B * PAGES * DV // LIST_ROWS], U16, name="value_list")
@@ -52,28 +51,29 @@ def tile_attend_pkv4_soft_draft_gate_kernel(
             cols = PAGES * DV // LIST_ROWS
             return value_list[:, b * cols : (b + 1) * cols]
 
-        kw_pool = sb("kw_pool", [P, T], U32)
         ks_pool = sb("ks_pool", [P, T], U8)
-        vw_pool = sb("vw_pool", [P, POOL_PAGES * DV], U32)
         vsc_pool = sb("vsc_pool", [P, POOL_PAGES * DV], U8)
-        vs_pool = sb("vs_pool", [P, T], F32)
-        pos_pool = sb("pos_pool", [P, T], F32)
-        q_raw = sb("q_raw", [P, B * PASSES, PACK, NQ], F32)
-        og_sb = sb("og_sb", [P, B, DV], F32)
-        qpos_sb = [sb(f"qpos{b}", [P, 1], F32) for b in range(B)]
-        ks_high = [sb(f"ks_high{b}", [P, N], U8) for b in range(B)]
+        qpos_sb = sb("qpos_sb", [P, B], F32)
+        ks_high = sb("ks_high", [P, B * N], U8)
 
+        nc.gpsimd.memset(vsc_pool[:].bitcast(I32), 0)
         nc.vector.memset(ks_pool[:].bitcast(I32), 0)
-        nc.vector.memset(vsc_pool[:].bitcast(I32), 0)
+        nc.gpsimd.memset(ks_high[:].bitcast(I32), 0)
+        ones = sb("ones", [P, P], F32, tag="kw_pool")
+        nc.gpsimd.memset(ones[:], 1.0)
         ident = sb("ident", [P, P], F32)
-        make_identity(nc, ident[:])
-        for b in range(B):
-            nc.gpsimd.memset(ks_high[b][:].bitcast(I32), 0)
-
-        nc.sync.dma_start(
-            vw_pool[:].bitcast(I32).rearrange("p (u e) -> p u e", u=POOL_PAGES),
-            v_words.rearrange("u p e r -> p u (e r)").bitcast(I32),
+        nc.gpsimd.affine_select(
+            out=ident[:], in_=ones[:], pattern=[[-1, P]], compare_op=ALU.is_equal, fill=0.0, base=0, channel_multiplier=1
         )
+        kw_pool = sb("kw_pool", [P, T], U32)
+
+        with nc.allow_non_contiguous_dma(reason="one place a query row and sequence"):
+            nc.sync.dma_start(qpos_sb[:], qpos.rearrange("b q o -> q (b o)"))
+        for quad in range(4):
+            nc.sync.dma_start(
+                vsc_pool[32 * quad : 32 * quad + 4, :].bitcast(I32).rearrange("f (u e) -> f u e", u=POOL_PAGES),
+                v_scales[:, 4 * quad : 4 * quad + 4, :].rearrange("u f e -> f u e").bitcast(I32),
+            )
         for quad in range(4):
             nc.sync.dma_start(
                 ks_pool[32 * quad : 32 * quad + 4 * PASSES, :].bitcast(I32),
@@ -82,28 +82,20 @@ def tile_attend_pkv4_soft_draft_gate_kernel(
         nc.sync.dma_start(
             kw_pool[:].bitcast(I32), k_words[0].rearrange("p t r -> p (t r)").bitcast(I32)
         )
+
+        vsc = sb("vsc", [P, B * PAGES * DV], U8)
+        nc.vector.tensor_copy(vsc[:], vsc_pool[:].indirect(value_list[:]))
+        q_raw = sb("q_raw", [P, B * PASSES, PACK, NQ], F32, tag="vsc_pool")
         nc.sync.dma_start(
             q_raw[:].rearrange("p c j q -> p c (j q)"),
             qT.rearrange("b (g p j) q -> p (b g) (j q)", g=PASSES, j=PACK),
         )
+
+        ks = sb("ks", [P, B * N], U8)
+        nc.vector.tensor_copy(ks[:], ks_pool[:].indirect(key_list[:]))
+        pos_pool = sb("pos_pool", [P, T], F32, tag="ks_pool")
         nc.sync.dma_start(pos_pool[:], pos)
-        for b in range(B):
-            nc.sync.dma_start(qpos_sb[b][:], qpos[b])
-        nc.sync.dma_start(vs_pool[:], vs)
-        nc.sync.dma_start(og_sb[:], og.rearrange("b q e -> q b e"))
-        for quad in range(4):
-            nc.sync.dma_start(
-                vsc_pool[32 * quad : 32 * quad + 4, :].bitcast(I32).rearrange("f (u e) -> f u e", u=POOL_PAGES),
-                v_scales[:, 4 * quad : 4 * quad + 4, :].rearrange("u f e -> f u e").bitcast(I32),
-            )
-
-        vw = sb("vw", [P, B * PAGES * DV], U32)
-        nc.vector.tensor_copy(vw[:], vw_pool[:].indirect(value_list[:]))
-
-        ks = [sb(f"ks{b}", [P, N], U8) for b in range(B)]
-        for b in range(B):
-            nc.vector.tensor_copy(ks[b][:], ks_pool[:].indirect(keys_of(b)))
-            nc.scalar.dma_start(ks_high[b][0:112, :].bitcast(I32), ks[b][4:116, :].bitcast(I32))
+        nc.sync.dma_start(ks_high[0:112, :].bitcast(I32), ks[4:116, :].bitcast(I32))
 
         q_bf = sb("q_bf", [P, B * PASSES, NQ, PACK], BF16)
         for c in range(B * PASSES):
@@ -111,6 +103,8 @@ def tile_attend_pkv4_soft_draft_gate_kernel(
                 q_bf[:, c].rearrange("p (a i) j -> p a j i", i=4),
                 q_raw[:, c].rearrange("p j (a i) -> p a j i", i=4),
             )
+        vs_pool = sb("vs_pool", [P, T], F32, tag="vsc_pool")
+        nc.sync.dma_start(vs_pool[:], vs)
         q_codes = sb("q_codes", [P, B * PASSES * NQ], U32)
         q_scales = sb("q_scales", [P, B * PASSES * NQ], U8)
 
@@ -126,7 +120,7 @@ def tile_attend_pkv4_soft_draft_gate_kernel(
             )
 
         def score(b):
-            planes = [ks[b], ks_high[b]]
+            planes = [ks, ks_high]
             for h in range(PAGES):
                 for g in range(PASSES):
                     cols = slice((b * PASSES + g) * NQ, (b * PASSES + g + 1) * NQ)
@@ -135,7 +129,7 @@ def tile_attend_pkv4_soft_draft_gate_kernel(
                         lhsT=q_codes[:, cols].bitcast(FP8X4),
                         lhsT_scale=q_scales[:, cols],
                         rhs=k4[b][:, g, 2 * PAGE * h : 2 * PAGE * (h + 1)].bitcast(FP4X4),
-                        rhs_scale=planes[g][:, PAGE * h : PAGE * (h + 1)],
+                        rhs_scale=planes[g][:, b * N + PAGE * h : b * N + PAGE * (h + 1)],
                         start=(g == 0),
                         stop=(g == PASSES - 1),
                     )
@@ -144,18 +138,25 @@ def tile_attend_pkv4_soft_draft_gate_kernel(
         nc.vector.quantize_mx(
             out=q_codes[:].bitcast(FP8X4), scales=q_scales[:], in_=q_bf[:].rearrange("p c q j -> p (c q j)")
         )
+        og_sb = sb("og_sb", [P, B, DV], F32, tag="kw0")
+        nc.sync.dma_start(og_sb[:], og.rearrange("b q e -> q b e"))
         score(0)
         gather_keys(1)
         score(1)
+        vw_pool = sb("vw_pool", [P, POOL_PAGES * DV], U32, tag="kw_pool")
+        nc.sync.dma_start(
+            vw_pool[:].bitcast(I32).rearrange("p (u e) -> p u e", u=POOL_PAGES),
+            v_words.rearrange("u p e r -> p u (e r)").bitcast(I32),
+        )
 
         ahead = []
+        origin = sb("origin", [P, B], F32)
+        nc.scalar.mul(origin[:], qpos_sb[:], -STEEP)
         for b in range(B):
             places = sb(f"places{b}", [P, N], F32)
             nc.vector.tensor_copy(places[:], pos_pool[:].indirect(keys_of(b)))
-            origin = sb(f"origin{b}", [P, 1], F32)
-            nc.scalar.mul(origin[:], qpos_sb[b][:], -STEEP)
             pen = sb(f"ahead{b}", [P, N], F32)
-            nc.scalar.activation(pen[:], places[:], ACT.Relu, bias=origin[:], scale=STEEP)
+            nc.scalar.activation(pen[:], places[:], ACT.Relu, bias=origin[:, b : b + 1], scale=STEEP)
             ahead.append(pen)
 
         gate = sb("gate", [P, B, DV], F32)
@@ -165,9 +166,8 @@ def tile_attend_pkv4_soft_draft_gate_kernel(
 
         p = [sb(f"p{b}", [P, N], F32) for b in range(B)]
         sums = [sb(f"sums{b}", [P, PAGES], F32) for b in range(B)]
-        sizes = [sb(f"sizes{b}", [P, N], F32) for b in range(B)]
-        vsc = [sb(f"vsc{b}", [P, PAGES * DV], U8) for b in range(B)]
-        w = [[sb(f"w{b}{h}", [P, PAGE], BF16) for h in range(PAGES)] for b in range(B)]
+        vw = {}
+        w = [[sb(f"w{b}{h}", [P, PAGE], F32) for h in range(PAGES)] for b in range(B)]
         wt = [[sb(f"wt{b}{h}", [P, NQ, PACK], BF16) for h in range(PAGES)] for b in range(B)]
         y = [psum.tile([P, DV], F32, name=f"y{b}") for b in range(B)]
 
@@ -185,39 +185,41 @@ def tile_attend_pkv4_soft_draft_gate_kernel(
                     p[b][:, cols], neg[:, cols], ACT.Exp, bias=neg_max[:], scale=-1.0, accum_out=sums[b][:, h : h + 1]
                 )
 
-        def gather_sizes(b):
-            nc.vector.tensor_copy(sizes[b][:], vs_pool[:].indirect(keys_of(b)))
-
-        def gather_value_scales(b):
-            nc.vector.tensor_copy(vsc[b][:], vsc_pool[:].indirect(values_of(b)))
+        def gather_values(b):
+            vw[b] = sb(f"vw{b}", [P, PAGES * DV], U32, tag=f"wt0{b}")
+            nc.vector.tensor_copy(vw[b][:], vw_pool[:].indirect(values_of(b)))
 
         def weigh(b):
             for h in range(PAGES):
                 cols = slice(PAGE * h, PAGE * (h + 1))
-                nc.vector.tensor_tensor(w[b][h][:], p[b][:, cols], sizes[b][:, cols], ALU.mult)
-                pairs = w[b][h][:].bitcast(F32)
-                turned = psum.tile([P, 2, NQ], F32, name=f"turned{h}")
-                for u in range(2):
-                    nc.tensor.transpose(turned[:, u, :], pairs[:, u : PAGE // 2 : 2], ident[:])
-                nc.scalar.copy(
-                    wt[b][h][:].rearrange("p q j -> p (q j)").bitcast(F32).rearrange("p (q u) -> p q u", u=2),
-                    turned[:].rearrange("p u q -> p q u"),
-                )
+                first = (b * PAGES + h) * PAGE // LIST_ROWS
+                page_list = key_list[:, first : first + PAGE // LIST_ROWS]
+                nc.vector.tensor_tensor(w[b][h][:], vs_pool[:].indirect(page_list), p[b][:, cols], ALU.mult)
+                turned = psum.tile([P, PACK, NQ], F32, name=f"turned{h}")
+                for j in range(PACK):
+                    nc.tensor.transpose(turned[:, j, :], w[b][h][:, j:PAGE:PACK], ident[:])
+                nc.scalar.copy(wt[b][h][:], turned[:].rearrange("p j q -> p q j"))
+
+        quantised = {}
+
+        def quantise_weights(b, h):
+            w_codes = sb(f"w_codes{b}{h}", [P, NQ], U32)
+            w_scales = sb(f"w_scales{b}{h}", [P, NQ], U8)
+            nc.vector.quantize_mx(
+                out=w_codes[:].bitcast(FP8X4), scales=w_scales[:], in_=wt[b][h][:].rearrange("p q j -> p (q j)")
+            )
+            quantised[b, h] = (w_codes, w_scales)
 
         def multiply(b):
             for h in range(PAGES):
-                w_codes = sb(f"w_codes{b}{h}", [P, NQ], U32)
-                w_scales = sb(f"w_scales{b}{h}", [P, NQ], U8)
-                nc.vector.quantize_mx(
-                    out=w_codes[:].bitcast(FP8X4), scales=w_scales[:], in_=wt[b][h][:].rearrange("p q j -> p (q j)")
-                )
+                w_codes, w_scales = quantised[b, h]
                 page = b * PAGES + h
                 nc.tensor.matmul_mx(
                     out=y[b][:],
                     lhsT=w_codes[:].bitcast(FP8X4),
                     lhsT_scale=w_scales[:],
-                    rhs=vw[:, page * DV : (page + 1) * DV].bitcast(FP8X4),
-                    rhs_scale=vsc[b][:, h * DV : (h + 1) * DV],
+                    rhs=vw[b][:, h * DV : (h + 1) * DV].bitcast(FP8X4),
+                    rhs_scale=vsc[:, page * DV : (page + 1) * DV],
                     start=(h == 0),
                     stop=(h == PAGES - 1),
                 )
@@ -227,19 +229,20 @@ def tile_attend_pkv4_soft_draft_gate_kernel(
             nc.scalar.activation(total[:], sums[b][:, 0:1], ACT.Identity, bias=sums[b][:, 1:2])
             inverse = sb(f"inverse{b}", [P, 1], F32)
             nc.vector.reciprocal(inverse[:], total[:])
-            result = sb(f"result{b}", [P, DV], F32)
+            result = sb(f"result{b}", [P, DV], F32, tag=["wt11", "result1"][b])
             nc.vector.scalar_tensor_tensor(result[:], y[b][:], inverse[:], gate[:, b, :], ALU.mult, ALU.mult)
             nc.sync.dma_start(out[b], result[:])
 
         softmax(0)
-        gather_sizes(0)
         softmax(1)
         weigh(0)
-        gather_sizes(1)
-        gather_value_scales(0)
-        multiply(0)
         weigh(1)
-        gather_value_scales(1)
-        finish(0)
+        for b in range(B):
+            quantise_weights(0, b)
+            gather_values(b)
+        multiply(0)
+        for h in range(PAGES):
+            quantise_weights(1, h)
         multiply(1)
+        finish(0)
         finish(1)

@@ -14,6 +14,7 @@ MASKED = 30000.0
 STEEP = 2.0 ** 64
 
 FLOPS = 2 * B * NQ * N * (D + DV)
+BYTES = 4 * B * NQ * (D + 2 * DV + 1) + T * (D // 2 + D // 32 + DV + DV // 32 + 8) + 2 * P * (B * N + B * PAGES * DV) // LIST_ROWS
 
 F32 = mybir.dt.float32
 BF16 = mybir.dt.bfloat16
@@ -33,6 +34,7 @@ def tile_attend_pkv4_soft_draft_gate_kernel(
     nc = tc.nc
     with ExitStack() as ctx:
         keep = ctx.enter_context(tc.tile_pool(name="keep", bufs=1))
+        shared = ctx.enter_context(tc.tile_pool(name="shared", bufs=1))
         psum = ctx.enter_context(tc.psum_pool(name="psum", bufs=1))
 
         def sb(name, shape, dtype, tag=None):
@@ -53,22 +55,26 @@ def tile_attend_pkv4_soft_draft_gate_kernel(
 
         ks_pool = sb("ks_pool", [P, T], U8)
         vsc_pool = sb("vsc_pool", [P, POOL_PAGES * DV], U8)
-        qpos_sb = sb("qpos_sb", [P, B], F32)
         ks_high = sb("ks_high", [P, B * N], U8)
 
         nc.gpsimd.memset(vsc_pool[:].bitcast(I32), 0)
         nc.vector.memset(ks_pool[:].bitcast(I32), 0)
         nc.gpsimd.memset(ks_high[:].bitcast(I32), 0)
-        ones = sb("ones", [P, P], F32, tag="kw_pool")
+        def placed(name, shape, dtype, offset):
+            return shared.tile(shape, dtype, name=name, align_bytes=64, offset=offset)
+
+        ones = placed("ones", [P, P], F32, 0)
         nc.gpsimd.memset(ones[:], 1.0)
         ident = sb("ident", [P, P], F32)
         nc.gpsimd.affine_select(
             out=ident[:], in_=ones[:], pattern=[[-1, P]], compare_op=ALU.is_equal, fill=0.0, base=0, channel_multiplier=1
         )
-        kw_pool = sb("kw_pool", [P, T], U32)
+        RUN = T // P
+        pos_row = placed("pos_row", [P, RUN], F32, 0)
+        vs_row = placed("vs_row", [P, RUN], F32, 128)
+        qpos_sb = placed("qpos_sb", [P, B], F32, 256)
+        kw_pool = placed("kw_pool", [P, T], U32, 384)
 
-        with nc.allow_non_contiguous_dma(reason="one place a query row and sequence"):
-            nc.sync.dma_start(qpos_sb[:], qpos.rearrange("b q o -> q (b o)"))
         for quad in range(4):
             nc.sync.dma_start(
                 vsc_pool[32 * quad : 32 * quad + 4, :].bitcast(I32).rearrange("f (u e) -> f u e", u=POOL_PAGES),
@@ -79,6 +85,10 @@ def tile_attend_pkv4_soft_draft_gate_kernel(
                 ks_pool[32 * quad : 32 * quad + 4 * PASSES, :].bitcast(I32),
                 k_scales[:, 4 * quad : 4 * quad + 4, :].bitcast(I32),
             )
+        nc.sync.dma_start(pos_row[:], pos[0].rearrange("(p j) -> p j", j=RUN))
+        nc.sync.dma_start(vs_row[:], vs[0].rearrange("(p j) -> p j", j=RUN))
+        with nc.allow_non_contiguous_dma(reason="one place a query row and sequence"):
+            nc.sync.dma_start(qpos_sb[:], qpos.rearrange("b q o -> q (b o)"))
         nc.sync.dma_start(
             kw_pool[:].bitcast(I32), k_words[0].rearrange("p t r -> p (t r)").bitcast(I32)
         )
@@ -93,9 +103,22 @@ def tile_attend_pkv4_soft_draft_gate_kernel(
 
         ks = sb("ks", [P, B * N], U8)
         nc.vector.tensor_copy(ks[:], ks_pool[:].indirect(key_list[:]))
-        pos_pool = sb("pos_pool", [P, T], F32, tag="ks_pool")
-        nc.sync.dma_start(pos_pool[:], pos)
         nc.sync.dma_start(ks_high[0:112, :].bitcast(I32), ks[4:116, :].bitcast(I32))
+
+        def spread(name, row):
+            pool_tile = sb(name, [P, T], F32)
+            by_run = pool_tile[:].rearrange("m (p j) -> m p j", j=RUN)
+            for a in range(RUN // PACK):
+                bank = psum.tile([P, PACK, P], F32, name=f"{name}{a}", tag=f"scores{a % 4 // 2}{a % 2}")
+                for i in range(PACK):
+                    j = a * PACK + i
+                    nc.tensor.transpose(bank[:, i, :], row[:, j : j + 1].to_broadcast([P, P]), ident[:])
+                nc.scalar.activation(
+                    by_run[:, :, a * PACK : (a + 1) * PACK], bank[:].rearrange("m i p -> m p i"), ACT.Copy
+                )
+            return pool_tile
+
+        pos_pool = spread("pos_pool", pos_row)
 
         q_bf = sb("q_bf", [P, B * PASSES, NQ, PACK], BF16)
         for c in range(B * PASSES):
@@ -103,8 +126,7 @@ def tile_attend_pkv4_soft_draft_gate_kernel(
                 q_bf[:, c].rearrange("p (a i) j -> p a j i", i=4),
                 q_raw[:, c].rearrange("p j (a i) -> p a j i", i=4),
             )
-        vs_pool = sb("vs_pool", [P, T], F32, tag="vsc_pool")
-        nc.sync.dma_start(vs_pool[:], vs)
+        vs_pool = spread("vs_pool", vs_row)
         q_codes = sb("q_codes", [P, B * PASSES * NQ], U32)
         q_scales = sb("q_scales", [P, B * PASSES * NQ], U8)
 
@@ -143,7 +165,7 @@ def tile_attend_pkv4_soft_draft_gate_kernel(
         score(0)
         gather_keys(1)
         score(1)
-        vw_pool = sb("vw_pool", [P, POOL_PAGES * DV], U32, tag="kw_pool")
+        vw_pool = sb("vw_pool", [P, POOL_PAGES * DV], U32, tag="ks_pool")
         nc.sync.dma_start(
             vw_pool[:].bitcast(I32).rearrange("p (u e) -> p u e", u=POOL_PAGES),
             v_words.rearrange("u p e r -> p u (e r)").bitcast(I32),
@@ -153,7 +175,7 @@ def tile_attend_pkv4_soft_draft_gate_kernel(
         origin = sb("origin", [P, B], F32)
         nc.scalar.mul(origin[:], qpos_sb[:], -STEEP)
         for b in range(B):
-            places = sb(f"places{b}", [P, N], F32)
+            places = sb(f"places{b}", [P, N], F32, tag=["vsc_pool", "q_bf"][b])
             nc.vector.tensor_copy(places[:], pos_pool[:].indirect(keys_of(b)))
             pen = sb(f"ahead{b}", [P, N], F32)
             nc.scalar.activation(pen[:], places[:], ACT.Relu, bias=origin[:, b : b + 1], scale=STEEP)

from contextlib import ExitStack

import concourse.mybir as mybir

B, N, T, D, DV, NQ = 2, 1024, 4096, 1024, 256, 128
PAGE = 512
P = 128
PACK = 4
PASSES = D // PAGE
PAGES = N // PAGE
POOL_PAGES = T // PAGE
LIST_ROWS = 16
MASKED = 30000.0
STEEP = 2.0 ** 64

FLOPS = 2 * B * NQ * N * (D + DV)
BYTES = 4 * B * NQ * (D + 2 * DV + 1) + T * (D // 2 + D // 32 + DV + DV // 32 + 8) + 2 * P * (B * N + B * PAGES * DV) // LIST_ROWS

F32 = mybir.dt.float32
BF16 = mybir.dt.bfloat16
I32 = mybir.dt.int32
U32 = mybir.dt.uint32
U16 = mybir.dt.uint16
U8 = mybir.dt.uint8
FP8X4 = mybir.dt.float8_e4m3fn_x4
FP4X4 = mybir.dt.float4_e2m1fn_x4
ALU = mybir.AluOpType
ACT = mybir.ActivationFunctionType


def tile_attend_pkv4_soft_draft_gate_kernel(
    tc, qT, k_words, k_scales, v_words, v_scales, vs, pos, qpos, og, offs, voffs, out
):
    nc = tc.nc
    with ExitStack() as ctx:
        keep = ctx.enter_context(tc.tile_pool(name="keep", bufs=1))
        shared = ctx.enter_context(tc.tile_pool(name="shared", bufs=1))
        psum = ctx.enter_context(tc.psum_pool(name="psum", bufs=1))

        def sb(name, shape, dtype, tag=None):
            return keep.tile(shape, dtype, name=name, tag=tag or name, align_bytes=64)

        key_list = keep.tile([P, B * N // LIST_ROWS], U16, name="key_list")
        value_list = keep.tile([P, B * PAGES * DV // LIST_ROWS], U16, name="value_list")
        nc.sync.dma_start(value_list[:], voffs)
        nc.sync.dma_start(key_list[:], offs)

        def keys_of(b):
            cols = N // LIST_ROWS
            return key_list[:, b * cols : (b + 1) * cols]

        def values_of(b):
            cols = PAGES * DV // LIST_ROWS
            return value_list[:, b * cols : (b + 1) * cols]

        ks_pool = sb("ks_pool", [P, T], U8)
        vsc_pool = sb("vsc_pool", [P, POOL_PAGES * DV], U8)
        ks_high = sb("ks_high", [P, B * N], U8)

        nc.gpsimd.memset(vsc_pool[:].bitcast(I32), 0)
        nc.vector.memset(ks_pool[:].bitcast(I32), 0)
        nc.gpsimd.memset(ks_high[:].bitcast(I32), 0)
        def placed(name, shape, dtype, offset):
            return shared.tile(shape, dtype, name=name, align_bytes=64, offset=offset)

        ones = placed("ones", [P, P], F32, 0)
        nc.gpsimd.memset(ones[:], 1.0)
        ident = sb("ident", [P, P], F32)
        nc.gpsimd.affine_select(
            out=ident[:], in_=ones[:], pattern=[[-1, P]], compare_op=ALU.is_equal, fill=0.0, base=0, channel_multiplier=1
        )
        RUN = T // P
        pos_row = placed("pos_row", [P, RUN], F32, 0)
        vs_row = placed("vs_row", [P, RUN], F32, 128)
        qpos_sb = placed("qpos_sb", [P, B], F32, 256)
        kw_pool = placed("kw_pool", [P, T], U32, 384)

        for quad in range(4):
            nc.sync.dma_start(
                vsc_pool[32 * quad : 32 * quad + 4, :].bitcast(I32).rearrange("f (u e) -> f u e", u=POOL_PAGES),
                v_scales[:, 4 * quad : 4 * quad + 4, :].rearrange("u f e -> f u e").bitcast(I32),
            )
        for quad in range(4):
            nc.sync.dma_start(
                ks_pool[32 * quad : 32 * quad + 4 * PASSES, :].bitcast(I32),
                k_scales[:, 4 * quad : 4 * quad + 4, :].bitcast(I32),
            )
        nc.sync.dma_start(pos_row[:], pos[0].rearrange("(p j) -> p j", j=RUN))
        nc.sync.dma_start(vs_row[:], vs[0].rearrange("(p j) -> p j", j=RUN))
        with nc.allow_non_contiguous_dma(reason="one place a query row and sequence"):
            nc.sync.dma_start(qpos_sb[:], qpos.rearrange("b q o -> q (b o)"))
        nc.sync.dma_start(
            kw_pool[:].bitcast(I32), k_words[0].rearrange("p t r -> p (t r)").bitcast(I32)
        )

        vsc = sb("vsc", [P, B * PAGES * DV], U8)
        nc.vector.tensor_copy(vsc[:], vsc_pool[:].indirect(value_list[:]))
        q_raw = sb("q_raw", [P, B * PASSES, PACK, NQ], F32, tag="vsc_pool")
        nc.sync.dma_start(
            q_raw[:].rearrange("p c j q -> p c (j q)"),
            qT.rearrange("b (g p j) q -> p (b g) (j q)", g=PASSES, j=PACK),
        )

        ks = sb("ks", [P, B * N], U8)
        nc.vector.tensor_copy(ks[:], ks_pool[:].indirect(key_list[:]))
        nc.sync.dma_start(ks_high[0:112, :].bitcast(I32), ks[4:116, :].bitcast(I32))

        def spread(name, row):
            pool_tile = sb(name, [P, T], F32)
            by_run = pool_tile[:].rearrange("m (p j) -> m p j", j=RUN)
            for a in range(RUN // PACK):
                bank = psum.tile([P, PACK, P], F32, name=f"{name}{a}", tag=f"scores{a % 4 // 2}{a % 2}")
                for i in range(PACK):
                    j = a * PACK + i
                    nc.tensor.transpose(bank[:, i, :], row[:, j : j + 1].to_broadcast([P, P]), ident[:])
                nc.scalar.activation(
                    by_run[:, :, a * PACK : (a + 1) * PACK], bank[:].rearrange("m i p -> m p i"), ACT.Copy
                )
            return pool_tile

        pos_pool = spread("pos_pool", pos_row)

        q_bf = sb("q_bf", [P, B * PASSES, NQ, PACK], BF16)
        for c in range(B * PASSES):
            nc.scalar.copy(
                q_bf[:, c].rearrange("p (a i) j -> p a j i", i=4),
                q_raw[:, c].rearrange("p j (a i) -> p a j i", i=4),
            )
        vs_pool = spread("vs_pool", vs_row)
        q_codes = sb("q_codes", [P, B * PASSES * NQ], U32)
        q_scales = sb("q_scales", [P, B * PASSES * NQ], U8)

        kw = [sb(f"kw{b}", [P, N], U32) for b in range(B)]
        k4 = [sb(f"k4_{b}", [P, PASSES, 2 * N], U8) for b in range(B)]
        scores = [[psum.tile([P, PAGE], F32, name=f"scores{b}{h}") for h in range(PAGES)] for b in range(B)]

        def gather_keys(b):
            nc.vector.tensor_copy(kw[b][:], kw_pool[:].indirect(keys_of(b)))
            nc.vector.tensor_copy(
                k4[b][:].bitcast(U16),
                kw[b][:].bitcast(U16).rearrange("p (n g) -> p g n", g=PASSES),
            )

        def score(b):
            planes = [ks, ks_high]
            for h in range(PAGES):
                for g in range(PASSES):
                    cols = slice((b * PASSES + g) * NQ, (b * PASSES + g + 1) * NQ)
                    nc.tensor.matmul_mx(
                        out=scores[b][h][:],
                        lhsT=q_codes[:, cols].bitcast(FP8X4),
                        lhsT_scale=q_scales[:, cols],
                        rhs=k4[b][:, g, 2 * PAGE * h : 2 * PAGE * (h + 1)].bitcast(FP4X4),
                        rhs_scale=planes[g][:, b * N + PAGE * h : b * N + PAGE * (h + 1)],
                        start=(g == 0),
                        stop=(g == PASSES - 1),
                    )

        gather_keys(0)
        nc.vector.quantize_mx(
            out=q_codes[:].bitcast(FP8X4), scales=q_scales[:], in_=q_bf[:].rearrange("p c q j -> p (c q j)")
        )
        og_sb = sb("og_sb", [P, B, DV], F32, tag="kw0")
        nc.sync.dma_start(og_sb[:], og.rearrange("b q e -> q b e"))
        score(0)
        gather_keys(1)
        score(1)
        vw_pool = sb("vw_pool", [P, POOL_PAGES * DV], U32, tag="ks_pool")
        nc.sync.dma_start(
            vw_pool[:].bitcast(I32).rearrange("p (u e) -> p u e", u=POOL_PAGES),
            v_words.rearrange("u p e r -> p u (e r)").bitcast(I32),
        )

        ahead = []
        origin = sb("origin", [P, B], F32)
        nc.scalar.mul(origin[:], qpos_sb[:], -STEEP)
        for b in range(B):
            places = sb(f"places{b}", [P, N], F32, tag=["vsc_pool", "q_bf"][b])
            nc.vector.tensor_copy(places[:], pos_pool[:].indirect(keys_of(b)))
            pen = sb(f"ahead{b}", [P, N], F32)
            nc.scalar.activation(pen[:], places[:], ACT.Relu, bias=origin[:, b : b + 1], scale=STEEP)
            ahead.append(pen)

        gate = sb("gate", [P, B, DV], F32)
        half = sb("half", [P, B, DV], F32)
        nc.scalar.activation(half[:], og_sb[:], ACT.Tanh, scale=0.5)
        nc.scalar.activation(gate[:], half[:], ACT.Copy, bias=0.5, scale=0.5)

        p = [sb(f"p{b}", [P, N], F32) for b in range(B)]
        sums = [sb(f"sums{b}", [P, PAGES], F32) for b in range(B)]
        vw = {}
        w = [[sb(f"w{b}{h}", [P, PAGE], F32) for h in range(PAGES)] for b in range(B)]
        wt = [[sb(f"wt{b}{h}", [P, NQ, PACK], BF16) for h in range(PAGES)] for b in range(B)]
        y = [psum.tile([P, DV], F32, name=f"y{b}") for b in range(B)]

        def softmax(b):
            low = sb(f"low{b}", [P, N], F32)
            for h in range(PAGES):
                cols = slice(PAGE * h, PAGE * (h + 1))
                nc.vector.tensor_tensor(low[:, cols], ahead[b][:, cols], scores[b][h][:], ALU.subtract)
            neg = sb(f"neg{b}", [P, N], F32)
            neg_max = sb(f"neg_max{b}", [P, 1], F32)
            nc.vector.tensor_scalar(neg[:], low[:], MASKED, None, ALU.min, ALU.min, accum_out=neg_max[:])
            for h in range(PAGES):
                cols = slice(PAGE * h, PAGE * (h + 1))
                nc.scalar.activation(
                    p[b][:, cols], neg[:, cols], ACT.Exp, bias=neg_max[:], scale=-1.0, accum_out=sums[b][:, h : h + 1]
                )

        def gather_values(b):
            vw[b] = sb(f"vw{b}", [P, PAGES * DV], U32, tag=f"wt0{b}")
            nc.vector.tensor_copy(vw[b][:], vw_pool[:].indirect(values_of(b)))

        def weigh(b):
            for h in range(PAGES):
                cols = slice(PAGE * h, PAGE * (h + 1))
                first = (b * PAGES + h) * PAGE // LIST_ROWS
                page_list = key_list[:, first : first + PAGE // LIST_ROWS]
                nc.vector.tensor_tensor(w[b][h][:], vs_pool[:].indirect(page_list), p[b][:, cols], ALU.mult)
                turned = psum.tile([P, PACK, NQ], F32, name=f"turned{h}")
                for j in range(PACK):
                    nc.tensor.transpose(turned[:, j, :], w[b][h][:, j:PAGE:PACK], ident[:])
                nc.scalar.copy(wt[b][h][:], turned[:].rearrange("p j q -> p q j"))

        quantised = {}

        def quantise_weights(b, h):
            w_codes = sb(f"w_codes{b}{h}", [P, NQ], U32)
            w_scales = sb(f"w_scales{b}{h}", [P, NQ], U8)
            nc.vector.quantize_mx(
                out=w_codes[:].bitcast(FP8X4), scales=w_scales[:], in_=wt[b][h][:].rearrange("p q j -> p (q j)")
            )
            quantised[b, h] = (w_codes, w_scales)

        def multiply(b):
            for h in range(PAGES):
                w_codes, w_scales = quantised[b, h]
                page = b * PAGES + h
                nc.tensor.matmul_mx(
                    out=y[b][:],
                    lhsT=w_codes[:].bitcast(FP8X4),
                    lhsT_scale=w_scales[:],
                    rhs=vw[b][:, h * DV : (h + 1) * DV].bitcast(FP8X4),
                    rhs_scale=vsc[:, page * DV : (page + 1) * DV],
                    start=(h == 0),
                    stop=(h == PAGES - 1),
                )

        def finish(b):
            total = sb(f"total{b}", [P, 1], F32)
            nc.scalar.activation(total[:], sums[b][:, 0:1], ACT.Identity, bias=sums[b][:, 1:2])
            inverse = sb(f"inverse{b}", [P, 1], F32)
            nc.vector.reciprocal(inverse[:], total[:])
            result = sb(f"result{b}", [P, DV], F32, tag=["wt11", "result1"][b])
            nc.vector.scalar_tensor_tensor(result[:], y[b][:], inverse[:], gate[:, b, :], ALU.mult, ALU.mult)
            nc.sync.dma_start(out[b], result[:])

        softmax(0)
        softmax(1)
        weigh(0)
        weigh(1)
        for b in range(B):
            quantise_weights(0, b)
            gather_values(b)
        multiply(0)
        for h in range(PAGES):
            quantise_weights(1, h)
        multiply(1)
        finish(0)
        finish(1)
